import numpy as np
import ml_dtypes

BF16 = ml_dtypes.bfloat16


def bf(x):
    return np.asarray(x, np.float32).astype(BF16)


def f32(x):
    return np.asarray(x, np.float32)


def f64(x):
    return np.asarray(x).astype(np.float64)


def striped(idx):
    return np.tile(idx.reshape(-1, 16).T, (8, 1))


S, K, M, N, H = 1024, 128, 256, 256, 128


def sigmoid(v):
    return 1.0 / (1.0 + np.exp(-v))


def setup_inputs():
    return {"table": bf(np.random.standard_normal((K, S))), "w": bf(np.random.standard_normal((K, M)) / np.sqrt(K)), "offs": striped(np.sort(np.random.permutation(S)[:N]))}


def reference(table, w, offs):
    idx = offs[:16].T.reshape(-1)
    x = f64(table)[:, idx]
    y = f64(w).T @ x
    return y[:H] * sigmoid(y[H:])

@@ -1,0 +1,54 @@
+import concourse.mybir as mybir
+
+BF16, F32, U16 = mybir.dt.bfloat16, mybir.dt.float32, mybir.dt.uint16
+SIGMOID = mybir.ActivationFunctionType.Sigmoid
+MULT = mybir.AluOpType.mult
+
+P = 128
+S = 1024
+N = 256
+H = 128
+HALF = N // 2
+
+FLOPS = 2 * P * (2 * H) * N
+
+
+def tile_gather_matmul_kernel(tc, table, w, offs, out):
+    nc = tc.nc
+    with (
+        tc.tile_pool(name="held", bufs=1) as held,
+        tc.psum_pool(name="banks", bufs=1) as banks,
+    ):
+        tokens = held.tile([P, S], BF16, name="tokens")
+        nc.sync.dma_start(tokens[:], table)
+        offsets = held.tile([P, N // 16], U16, name="offsets")
+        nc.sync.dma_start(offsets[:], offs)
+        weights = held.tile([P, 2 * H], BF16, name="weights")
+        nc.scalar.dma_start(weights[:], w)
+
+        gate_banks = [banks.tile([H, HALF], F32, name="gate_bank%d" % h) for h in range(2)]
+        for h in range(2):
+            nc.tensor.matmul(
+                gate_banks[h][:],
+                weights[:, H : 2 * H],
+                tokens[:].indirect(offsets[:, h * (HALF // 16) : (h + 1) * (HALF // 16)]),
+                start=True,
+                stop=True,
+            )
+        value_banks = [banks.tile([H, HALF], F32, name="value_bank%d" % h) for h in range(2)]
+        for h in range(2):
+            nc.tensor.matmul(
+                value_banks[h][:],
+                weights[:, 0:H],
+                tokens[:].indirect(offsets[:, h * (HALF // 16) : (h + 1) * (HALF // 16)]),
+                start=True,
+                stop=True,
+            )
+
+        gate = held.tile([H, N], F32, name="gate")
+        gated = held.tile([H, N], F32, name="gated")
+        for h in range(2):
+            half = slice(h * HALF, (h + 1) * HALF)
+            nc.scalar.activation(gate[:, half], gate_banks[h][:], SIGMOID)
+            nc.vector.tensor_tensor(gated[:, half], value_banks[h][:], gate[:, half], MULT)
+            nc.sync.dma_start(out[:, half], gated[:, half])

@@ -20,11 +20,11 @@ def tile_gather_matmul_kernel(tc, table, w, offs, out):
         tc.psum_pool(name="banks", bufs=1) as banks,
     ):
         tokens = held.tile([P, S], BF16, name="tokens")
-        nc.sync.dma_start(tokens[:], table)
+        nc.scalar.dma_start(tokens[:], table)
+        weights = held.tile([P, 2 * H], BF16, name="weights")
+        nc.sync.dma_start(weights[:], w)
         offsets = held.tile([P, N // 16], U16, name="offsets")
         nc.sync.dma_start(offsets[:], offs)
-        weights = held.tile([P, 2 * H], BF16, name="weights")
-        nc.scalar.dma_start(weights[:], w)
 
         gate_banks = [banks.tile([H, HALF], F32, name="gate_bank%d" % h) for h in range(2)]
         for h in range(2):

import concourse.mybir as mybir

BF16, F32, U16 = mybir.dt.bfloat16, mybir.dt.float32, mybir.dt.uint16
SIGMOID = mybir.ActivationFunctionType.Sigmoid
MULT = mybir.AluOpType.mult

P = 128
S = 1024
N = 256
H = 128
HALF = N // 2

FLOPS = 2 * P * (2 * H) * N


def tile_gather_matmul_kernel(tc, table, w, offs, out):
    nc = tc.nc
    with (
        tc.tile_pool(name="held", bufs=1) as held,
        tc.psum_pool(name="banks", bufs=1) as banks,
    ):
        tokens = held.tile([P, S], BF16, name="tokens")
        nc.scalar.dma_start(tokens[:], table)
        weights = held.tile([P, 2 * H], BF16, name="weights")
        nc.sync.dma_start(weights[:], w)
        offsets = held.tile([P, N // 16], U16, name="offsets")
        nc.sync.dma_start(offsets[:], offs)

        gate_banks = [banks.tile([H, HALF], F32, name="gate_bank%d" % h) for h in range(2)]
        for h in range(2):
            nc.tensor.matmul(
                gate_banks[h][:],
                weights[:, H : 2 * H],
                tokens[:].indirect(offsets[:, h * (HALF // 16) : (h + 1) * (HALF // 16)]),
                start=True,
                stop=True,
            )
        value_banks = [banks.tile([H, HALF], F32, name="value_bank%d" % h) for h in range(2)]
        for h in range(2):
            nc.tensor.matmul(
                value_banks[h][:],
                weights[:, 0:H],
                tokens[:].indirect(offsets[:, h * (HALF // 16) : (h + 1) * (HALF // 16)]),
                start=True,
                stop=True,
            )

        gate = held.tile([H, N], F32, name="gate")
        gated = held.tile([H, N], F32, name="gated")
        for h in range(2):
            half = slice(h * HALF, (h + 1) * HALF)
            nc.scalar.activation(gate[:, half], gate_banks[h][:], SIGMOID)
            nc.vector.tensor_tensor(gated[:, half], value_banks[h][:], gate[:, half], MULT)
            nc.sync.dma_start(out[:, half], gated[:, half])
